import numpy as np, ml_dtypes
CORES = [3,11,19,27,35,43]
N = 6
BF = ml_dtypes.bfloat16
def f(rng, *shape):
    return (rng.standard_normal(shape, dtype=np.float32) * np.exp2(rng.integers(-2, 3, shape[:-1] + (1,)))).astype(BF)
def wide(rng, *shape):
    v = f(rng, *shape).astype(np.float32); k = shape[:-2] + (1, shape[-1])
    return (v * np.exp2(rng.integers(-6, 7, k)) * (rng.random(k) > 0.0625)).astype(BF)
P, NT, W, D = 1536, 192, 768, 32
def order(g):
    return range(N) if g < 4 else range(N - 1, -1, -1)
def places(ln):
    n = np.asarray(ln).reshape(-1, NT).astype(np.int64) + 1; m = len(n)
    t = np.repeat(np.tile(np.arange(NT), m), n.reshape(-1)).reshape(m, P)
    last = np.zeros((m, P), bool); last[np.arange(m)[:, None], np.add.accumulate(n, 1) - 1] = True
    return t, last
def steps(ln, ds):
    t, last = places(ln); m = len(t); src = np.arange(P) - np.take_along_axis(np.asarray(ds).reshape(m, NT).astype(np.int64), t, 1)
    e = np.zeros((m, P), np.int64); row = np.arange(m)
    for i in range(P):
        j = src[:, i]; e[:, i] = np.where(last[:, i], 0, 1 + np.where(j >= 0, e[row, np.maximum(j, 0)], 0))
    return e
def lengths(rng, at, big):
    n = np.zeros((N, 8, NT), np.int64)
    for r in range(N):
        for g in range(8):
            b = int(big[r, g]); rest = P - NT - b
            v = np.minimum(rng.multinomial(rest, rng.dirichlet(np.where(rng.random(NT - 1) < 0.25, 0.001, 1.0))), D)
            v = v + rng.multivariate_hypergeometric(D - v, rest - int(np.sum(v)))
            n[r, g] = np.insert(v, int(at[r, g]), b)
    return n
def starts(n):
    return np.add.accumulate(n + 1, 2) - n - 1
def distances(rng, n):
    s = starts(n); k = rng.integers(0, 4, n.shape)
    over = rng.integers(np.minimum(s, W - 1) + 1, W + 1)
    return np.where(k == 0, rng.integers(1, 9, n.shape), np.where(k == 3, over, rng.integers(1, W + 1, n.shape)))
def inside(rng, n, d, share):
    s = starts(n); d = np.array(d)
    for g in range(8):
        q = order(g)[0]; m = (d[q, g] > s[q, g]) & (s[q, g] > 0) & (rng.random(NT) < share)
        d[q, g] = np.where(m, rng.integers(1, np.maximum(s[q, g], 1) + 1), d[q, g])
    return d
def fit(n, d):
    d = np.array(d)
    for r in range(N):
        for g in range(8):
            e = []
            for t, (c, k) in enumerate(zip(n[r, g].tolist(), d[r, g].tolist())):
                s = len(e)
                for i in range(s, s + c): e.append(1 + (e[i - k] if i >= k else 0))
                if max(e[s:], default=0) > D:
                    d[r, g, t] = 1; e[s:] = range(1, c + 1)
                e.append(0)
    return d
def pack(rng, n, d):
    return {"ln": n.astype(np.int32), "ds": d.astype(np.int32), "le": f(rng, N, 128, NT)}
def setup_inputs(rng):
    n = lengths(rng, rng.integers(0, NT, (N, 8)), rng.integers(1, D + 1, (N, 8)))
    return pack(rng, n, fit(n, inside(rng, n, distances(rng, n), 0.75)))
def setup_inputs_deep(rng):
    at = np.where(rng.random((N, 8)) < 0.25, rng.choice(np.array([0, NT - 1]), (N, 8)), rng.integers(0, NT, (N, 8)))
    n = lengths(rng, at, np.full((N, 8), D)); d = np.where(rng.random(n.shape) < 0.5, rng.integers(1, 4, n.shape), distances(rng, n))
    d = inside(rng, n, d, 0.75); np.put_along_axis(d, at[:, :, None], 1, 2)
    return pack(rng, n, fit(n, d))
def setup_inputs_hops(rng):
    n = lengths(rng, rng.integers(0, NT, (N, 8)), rng.integers(1, D + 1, (N, 8)))
    return pack(rng, n, fit(n, inside(rng, n, rng.integers(W - 8, W + 1, n.shape), 1.0)))
def setup_inputs_ends(rng):
    at = rng.choice(np.array([0, NT - 1]), (N, 8)); at[:, :2] = 0
    n = lengths(rng, at, rng.integers(2, D + 1, (N, 8))); n[rng.integers(0, N)] = P // NT - 1
    s = starts(n); d = np.choose(rng.integers(0, 6, n.shape), [s * 0 + W, s * 0 + 1, s, s + 1, s + n, n])
    d = inside(rng, n, np.minimum(np.maximum(d, 1), W), 0.5); d[:, 0, 0] = W; d[:, 1, 0] = 1
    return pack(rng, n, fit(n, d))
def setup_inputs_long(rng):
    at = rng.integers(0, NT, (N, 8)); k = rng.integers(P // D, W + 1, (N, 8)); u = rng.integers(0, 3, (N, 8)); k = np.where(u == 0, P // D, np.where(u == 1, W, k))
    for g in range(8):
        q = order(g)[0]; at[q, g] = NT - 1; k[q, g] = rng.integers(P // D, min(W, NT - 1) + 1)
    n = np.zeros((N, 8, NT), np.int64); np.put_along_axis(n, at[:, :, None], P - NT, 2)
    d = rng.integers(1, W + 1, n.shape); np.put_along_axis(d, at[:, :, None], k[:, :, None], 2)
    return pack(rng, n, d)
def setup_inputs_spread(rng):
    d = setup_inputs(rng); d["le"] = wide(rng, N, 128, NT); return d
def check_inputs(d):
    bad = []; a = np.asarray(d["ln"]).astype(np.int64); b = np.asarray(d["ds"]).astype(np.int64)
    if (a < 0).any() or (np.sum(a, 2) + NT != P).any(): bad.append("lengths")
    if (b < 1).any() or (b > W).any(): bad.append("distances")
    if not bad and (steps(a, b) > D).any(): bad.append("steps")
    if not np.isfinite(np.asarray(d["le"]).astype(np.float32)).all(): bad.append("finite")
    return bad
def reference(ln, ds, le):
    y = np.zeros((N, 128, P), BF); t, last = places(ln); t = t.reshape(N, 8, P); last = last.reshape(N, 8, P)
    for g in range(8):
        buf = np.zeros((W + P, 16), BF)
        for r in order(g):
            a = np.ascontiguousarray(le[r, 16 * g:16 * g + 16].T); k = ds[r, g][t[r, g]].tolist(); tk = t[r, g].tolist(); own = last[r, g].tolist()
            for i in range(P):
                buf[W + i] = a[tk[i]] if own[i] else buf[W + i - k[i]]
            y[r, 16 * g:16 * g + 16] = buf[W:].T
            buf[:W] = buf[P:]
    return {"y": y}

@@ -1,0 +1,262 @@
+from concourse.bass import DstId, RemoteDMATransfer
+from concourse.mybir import AluOpType, ActivationFunctionType
+
+N, P, NT, W = 6, 1536, 192, 768
+H = NT + W
+C = NT // 16
+LW = W // 16
+SCRATCH = {
+    "lnb": ("sbuf", [128, C], "int32"), "dsb": ("sbuf", [128, C], "int32"),
+    "n1": ("sbuf", [128, C], "float32"), "sc": ("sbuf", [128, C], "float32"), "sch": ("sbuf", [128, 1], "float16"),
+    "ex": ("sbuf", [128, C], "float32"), "zi": ("sbuf", [128, C], "float32"), "zc": ("sbuf", [128, C], "float32"),
+    "zd": ("sbuf", [128, C], "float32"), "u": ("sbuf", [128, C], "float32"), "pre": ("sbuf", [128, C], "float32"),
+    "rs": ("sbuf", [128, 1], "float32"),
+    "lasts": ("sbuf", [128, C], "uint16"), "firsts": ("sbuf", [128, C], "uint16"), "ci": ("sbuf", [128, C], "int32"),
+    "cl": ("sbuf", [128, C], "uint16"),
+    "pi": ("sbuf", [128, 1], "int32"), "pj": ("sbuf", [128, 1], "int32"), "pm": ("sbuf", [128, 1], "float32"),
+    "p12": ("sbuf", [128, 1], "float32"), "p0": ("sbuf", [128, 1], "float32"),
+    "qi": ("sbuf", [128, NT], "float32"), "mk": ("sbuf", [128, NT], "float16"), "ml": ("sbuf", [128, NT], "float16"),
+    "c60": ("sbuf", [128, NT], "float16"), "yt": ("sbuf", [128, NT], "float16"), "gm": ("sbuf", [128, NT], "float16"),
+    "lt": ("sbuf", [128, NT], "float32"), "xd": ("sbuf", [128, NT], "float32"),
+    "ones": ("sbuf", [128, 144], "float16"), "fi": ("sbuf", [128, 144], "float16"), "f": ("sbuf", [128, 144], "float16"),
+    "b0": ("sbuf", [128, 128], "float16"), "bo": ("sbuf", [128, 128], "float16"), "tri": ("sbuf", [128, 128], "float16"),
+    "m": ("sbuf", [128, P], "float32"), "x": ("sbuf", [128, P], "float32"),
+    "r": ("sbuf", [128, P], "float16"),
+    "wa": ("sbuf", [128, H + P], "float32"), "wb": ("sbuf", [128, H + P], "float32"),
+    "la": ("sbuf", [128, P // 16], "uint16"), "lb": ("sbuf", [128, P // 16], "uint16"), "ol": ("sbuf", [128, P // 16], "uint16"),
+    "idi": ("sbuf", [128, LW], "int32"), "idl": ("sbuf", [128, LW], "uint16"),
+    "ll": ("sbuf", [128, N * LW], "uint16"), "cl5": ("sbuf", [128, N * LW], "uint16"),
+    "yo": ("sbuf", [128, P], "bfloat16"), "ye": ("sbuf", [128, P], "bfloat16"),
+    "dle": ("dram", [2, 128, NT // 2], "bfloat16"), "lel": ("dram", [N, 128, NT // 2], "bfloat16"),
+    "car": ("psum", [128, 512], "float32"), "rep": ("psum", [128, 512], "float32"),
+    "cva": ("psum", [128, 512], "float32"), "cvb": ("psum", [128, 512], "float32"),
+}
+for _k in range(N):
+    SCRATCH["sw%d" % _k] = ("sbuf", [128, H], "bfloat16")
+SEMAPHORES = ["cg", "cv", "cs", "cp", "dl", "dd", "dle", "lo", "lw", "st", "ls"] + ["ar%d" % k for k in range(N)] + ["la%d" % k for k in range(N)]
+
+
+def rank_program(g, core, T, topo):
+    rank = T.rank_of(core)
+    if rank is None:
+        return
+    A, CP = AluOpType, ActivationFunctionType.Copy
+    v, s, pe, sync, S = g.vector, g.scalar, g.tensor, g.sync, T.sem
+    queue = {"g": g, "v": v, "s": s, "p": pe, "y": sync}
+    cnt = {"g": 0, "v": 0, "s": 0, "p": 0}
+    seen = {}
+
+    def need(q, *deps):
+        for sem, val in deps:
+            if seen.get((q, sem), 0) < val:
+                queue[q].wait_ge(S[sem], val)
+                seen[(q, sem)] = val
+
+    def op(q, deps, ins):
+        need(q, *deps)
+        cnt[q] += 1
+        ins().then_inc(S["c" + q], 1)
+        return ("c" + q, cnt[q])
+
+    up, down = rank, N - 1 - rank
+    n = max(up, down)
+    mixed = up > 0 and down > 0
+    others = [r for r in range(N) if r != rank]
+    others.sort(key=lambda r: -abs(r - rank))
+    stage = [(k - (n - up), k - (n - down)) for k in range(n)]
+    stage = [(a if a >= 0 else None, N - 1 - b if b >= 0 else None) for a, b in stage]
+    own = None if mixed else stage[0].index(None)
+    sw = [T["sw%d" % k] for k in range(n + 1)]
+
+    def half(side):
+        return slice(64 * side, 64 * side + 64)
+
+    sync.dma_start(T.lnb[:], T.ln[:]).then_inc(S.dl, 16)
+    s.dma_start(T.dsb[:], T.ds[:]).then_inc(S.dd, 16)
+    sync.dma_start(T.dle[:], T.le[:]).then_inc(S.dle, 16)
+    sync.dma_start(sw[n][:, 0:NT], T.le[:]).then_inc(S.lo, 16)
+    if not mixed:
+        sync.dma_start(sw[0][half(own), 0:NT], T.le[half(own), :]).then_inc(S.lo, 16)
+
+    flag = {"allow_small_or_imprecise_dtypes": True}
+    ones = op("v", [], lambda: v.memset(T.ones[:], 1.0))
+    pi = op("g", [], lambda: g.iota(T.pi[:], [[1, 1]], 0, 1))
+    zb = op("v", [], lambda: v.memset(T.yo[:, 0:W], 0.0))
+    qi = op("g", [], lambda: g.iota(T.qi[:], [[0, C], [1, 16]], 0, 0, **flag))
+    zi = op("g", [], lambda: g.iota(T.zi[:], [[-1, C]], 1, 0, **flag))
+    ci = op("g", [], lambda: g.iota(T.ci[:], [[1, C]], 0, 0))
+    b0 = op("g", [ones], lambda: g.affine_select(T.b0[:], T.ones[:, 0:128], [[-16, 8], [0, 16]], A.is_ge, 0.0, 0, 1))
+    bo = op("g", [b0], lambda: g.affine_select(T.bo[:], T.b0[:], [[16, 8], [0, 16]], A.is_ge, 0.0, 15, -1))
+    tri = op("g", [bo], lambda: g.affine_select(T.tri[:], T.bo[:], [[1, 128]], A.is_gt, 0.0, 0, -1))
+    lt = op("g", [], lambda: g.iota(T.lt[:], [[1, C], [C, 16]], -H, 0, **flag))
+    fi = op("g", [ones], lambda: g.affine_select(T.fi[:], T.ones[:], [[-1, 144]], A.is_equal, 0.0, 16, 1))
+    ia = op("g", [], lambda: g.iota(T.wa[:, 0:H], [[1, H]], -H, 0, **flag))
+    if mixed:
+        idi = op("g", [], lambda: g.iota(T.idi[:], [[16, LW]], NT, 0))
+    m0 = op("s", [zb], lambda: s.activation(T.m[:, 0:W], T.yo[:, 0:W], CP, bias=4096.0))
+    m1 = op("s", [], lambda: s.activation(T.m[:, W:P], T.yo[:, 0:W], CP, bias=4096.0))
+    pj = op("v", [pi], lambda: v.tensor_scalar(T.pj[:], T.pi[:], 15, None, A.bitwise_and))
+    c60 = op("v", [], lambda: v.memset(T.c60[:], 60.0))
+    pm = op("v", [pj], lambda: v.tensor_copy(T.pm[:], T.pj[:]))
+    cl = op("v", [ci], lambda: v.tensor_copy(T.cl[:], T.ci[:]))
+    p12 = op("v", [pm], lambda: v.tensor_scalar(T.p12[:], T.pm[:], -float(C), None, A.mult))
+    f0 = op("v", [pm], lambda: v.tensor_scalar(T.p0[:], T.pm[:], 0.0, None, A.is_equal))
+    ml = op("v", [qi, pm], lambda: v.tensor_scalar(T.ml[:], T.qi[:], T.pm[:], None, A.is_gt))
+    zc = op("v", [zi, p12], lambda: v.tensor_scalar(T.zc[:], T.zi[:], T.p12[:], None, A.add))
+    mk = op("v", [qi], lambda: v.tensor_scalar(T.mk[:], T.qi[:], T.pm[:], None, A.is_equal))
+    x0 = op("v", [], lambda: v.memset(T.x[:, 0:W], 1.0))
+
+    n1 = op("v", [("dl", 16)], lambda: v.tensor_scalar(T.n1[:], T.lnb[:], 1.0, None, A.add))
+    zd = op("v", [zc, ("dd", 16)], lambda: v.tensor_tensor(T.zd[:], T.zc[:], T.dsb[:], A.subtract))
+    sc = op("v", [n1], lambda: v.tensor_tensor_scan(T.sc[:], T.n1[:], T.n1[:], 0.0, A.add, A.max))
+    u = op("v", [zd, n1], lambda: v.tensor_tensor(T.u[:], T.zd[:], T.n1[:], A.subtract))
+    pre = op("v", [sc, u], lambda: v.tensor_tensor(T.pre[:], T.u[:], T.sc[:], A.add))
+    ex = op("v", [sc], lambda: v.tensor_tensor(T.ex[:], T.sc[:], T.n1[:], A.subtract))
+    gm = op("v", [pre, cl, mk], lambda: v.tensor_tensor(T.gm[:], T.pre[:, 0:C].indirect(T.cl[:, 0:C]), T.mk[:], A.mult))
+    sch = op("s", [sc], lambda: s.activation(T.sch[:], T.sc[:, C - 1:C], CP))
+    yt = op("s", [sc, ml], lambda: s.activation(T.yt[:], T.ml[:], CP, scale=T.sc[:, C - 1:C]))
+    x1 = op("s", [x0], lambda: s.activation(T.x[:, W:P], T.x[:, 0:W], CP))
+    op("p", [bo, c60], lambda: pe.matmul(T.rep[:, 0:NT], T.bo[:], T.c60[:], True, False))
+    car = op("p", [tri, sch], lambda: pe.matmul(T.car[:, 0:1], T.tri[:], T.sch[:], True, True))
+    op("p", [yt], lambda: pe.matmul(T.rep[:, 0:NT], T.bo[:], T.yt[:], False, False))
+    rep = op("p", [gm], lambda: pe.matmul(T.rep[:, 0:NT], T.bo[:], T.gm[:], False, True))
+    lasts = op("v", [car, sc], lambda: v.tensor_scalar(T.lasts[:], T.sc[:], T.car[:, 0:1], -1.0, A.add, A.add))
+    firsts = op("v", [car, ex], lambda: v.tensor_scalar(T.firsts[:], T.ex[:], T.car[:, 0:1], None, A.add))
+    ms = op("v", [lasts, lt, m0, m1], lambda: v.tensor_copy(T.m[:, 0:P].indirect(T.lasts[:, 0:C]), T.lt[:]))
+    xd = op("s", [rep], lambda: s.activation(T.xd[:], T.rep[:, 0:NT], CP))
+    f = op("v", [f0, fi], lambda: v.tensor_scalar(T.f[:], T.fi[:], T.p0[:], None, A.mult))
+    xs = op("v", [firsts, xd, x1], lambda: v.tensor_copy(T.x[:, 0:P].indirect(T.firsts[:, 0:C]), T.xd[:]))
+    B = P // 3
+    ra = op("v", [ms, xs], lambda: v.tensor_tensor_scan(T.r[:, 0:B], T.x[:, 0:B], T.m[:, 0:B], -float(H + 1), A.add, A.min))
+    rs = op("v", [ra], lambda: v.tensor_copy(T.rs[:], T.r[:, B - 1:B]))
+    rb = op("v", [rs], lambda: v.tensor_tensor_scan(T.r[:, B:P], T.x[:, B:P], T.m[:, B:P], T.rs[:], A.add, A.min))
+    ib = op("s", [ia], lambda: s.activation(T.wb[:, 0:H], T.wa[:, 0:H], CP))
+
+    def conv(deps, out, a, b):
+        need("p", *deps)
+        for q in range(16):
+            t = op("p", [], lambda: pe.matmul(out[:, a // 16:b // 16], T.f[:, 16 - q:144 - q], T.r[:, a + q:b:16], q == 0, q == 15))
+        return t
+
+    def emit(dep, out, a, b, src):
+        return op("v", [dep], lambda: v.tensor_scalar(out[:, a:b], src[:, a:b], float(H), None, A.add))
+
+    def jump(deps, out, o, win, lst, a, b):
+        h = (a + b) // 2
+        e = o + 16 * (h - a)
+        z = win.shape[1]
+        t1 = op("v", deps, lambda: v.tensor_copy(out[:, o:e], win[:, 0:z].indirect(lst[:, a:h])))
+        t2 = op("s", deps, lambda: s.activation(out[:, e:o + 16 * (b - a)], win[:, 0:z].indirect(lst[:, h:b]), CP))
+        return [t1, t2]
+
+    full = P // 16
+    win, oth, lst, nxt = T.wa, T.wb, T.la, T.lb
+    conv([ra, f], T.cva, 0, B)
+    cp = conv([rb], T.cva, B, P)
+    ready = [op("s", [rb], lambda: s.activation(win[:, H + W:H + P], T.r[:, W:P], CP)),
+             op("v", [rb], lambda: v.tensor_copy(win[:, H:H + W], T.r[:, 0:W])), ia, ib]
+    z0 = op("v", [], lambda: v.memset(sw[0][:, NT:H], 0.0))
+    for k in range(n):
+        if None in stage[k] and (k or mixed):
+            z0 = op("v", [], lambda: v.memset(sw[k][half(stage[k].index(None)), 0:NT], 0.0))
+    if mixed:
+        idl = op("v", [idi], lambda: v.tensor_scalar(T.idl[:], T.idi[:], T.pm[:], None, A.add))
+        for k in range(n):
+            for side in range(2):
+                if stage[k][side] is None:
+                    z0 = op("v", [idl], lambda: v.tensor_copy(T.cl5[half(side), LW * k:LW * k + LW], T.idl[half(side), :]))
+    ready.append(emit(cp, lst, 0, full, T.cva))
+    for extra in (1, 1, 2):
+        t = jump(ready, T.r, 0, win, lst, 0, full)
+        cp = conv(t, T.cva, 0, P)
+        ready = [op("v", t[:1], lambda: v.tensor_copy(oth[:, H:H + W], T.r[:, 0:W])),
+                 op("s", t[1:], lambda: s.activation(oth[:, H + W:H + P], T.r[:, W:P], CP))]
+        win, oth = oth, win
+        for _ in range(extra):
+            ready = jump(ready, oth, H, win, lst, 0, full)
+            win, oth = oth, win
+        ready.append(emit(cp, nxt, 0, full, T.cva))
+        lst, nxt = nxt, lst
+    t = jump(ready, T.r, W, win, lst, LW, full)
+    cp = conv(t, T.cva, W, P)
+    t = jump(ready, T.r, 0, win, lst, 0, LW)
+    cq = conv(t, T.cvb, 0, W)
+    tail = emit(cp, T.ol, LW, full, T.cva)
+    te = []
+    if not mixed:
+        te += jump([tail, z0, ("lo", 32), ("lw", 16 * (up + down))], T.ye, W, sw[0], T.ol, LW, full)
+    head = emit(cq, T.ol, 0, LW, T.cvb)
+    if not mixed:
+        te += jump([head], T.ye, 0, sw[0], T.ol, 0, LW)
+
+    def ids(rs):
+        out = []
+        for r in rs:
+            a = topo.addr(T.cores[r])
+            out.append(DstId(rid=a[0], pnc=a[1]))
+        return out
+
+    def bits(engines):
+        return sum(1 << e for e in engines)
+
+    def shared(src):
+        es = [topo.engines(T.cores[src], T.cores[r]) for r in range(N) if r != src]
+        return [e for e in es[0] if all(e in x for x in es)]
+
+    def letter_engines(src):
+        e = shared(src)
+        if src == 0:
+            return e, []
+        if src == N - 1:
+            return [], e
+        return e[:len(e) // 2], e[len(e) // 2:]
+
+    trs = []
+    for side, rs in ((0, [r for r in others if r > rank]), (1, [r for r in others if r < rank])):
+        if rs:
+            trs.append(RemoteDMATransfer(dst_ids=ids(rs), dma_engine_mask=bits(letter_engines(rank)[side]), remote_sem=S["la%d" % rank],
+                                         srcs=[T.dle[side]], dsts=[T.lel[rank] for _ in rs]))
+    g.wait_ge(S.dle, 16)
+    g.remote_dma_fused(trs, local_sem=S.ls)
+    sent = sum(len(e) for e in letter_engines(rank))
+    need("g", tail)
+    g.remote_dma_fused([RemoteDMATransfer(dst_ids=ids(others), dma_engine_mask=bits(shared(rank)), remote_sem=S["ar%d" % rank],
+                                          srcs=[T.ol[:, LW:full]], dsts=[T.ll[:, LW * rank:LW * rank + LW] for _ in others])], local_sem=S.ls)
+    sent += len(shared(rank))
+
+    need("y", z0)
+    for k in range(n):
+        for side in range(2):
+            src = stage[k][side]
+            if src is not None:
+                need("y", ("la%d" % src, len(letter_engines(src)[side])))
+                sync.dma_start(sw[k][half(side), 0:NT], T.lel[src]).then_inc(S.lw, 16)
+    stored = 0
+    if not mixed:
+        need("y", *te)
+        sync.dma_start(T.y[half(own), :], T.ye[half(own), :]).then_inc(S.st, 16)
+        stored += 16
+
+    ready = [z0, ("lw", 16 * (up + down))]
+    for k in range(n):
+        if mixed:
+            for side in range(2):
+                src = stage[k][side]
+                if src is not None:
+                    ready.append(op("v", [("ar%d" % src, len(shared(src)))], lambda: v.tensor_copy(
+                        T.cl5[half(side), LW * k:LW * k + LW], T.ll[half(side), LW * src:LW * src + LW])))
+            lst, a = T.cl5, LW * k
+        else:
+            src = stage[k][1 - own]
+            ready.append(("ar%d" % src, len(shared(src))))
+            lst, a = T.ll, LW * src
+        ready = jump(ready, sw[k + 1], NT, sw[k], lst, a, a + LW)
+    ready += [head, ("lo", 16 if mixed else 32)]
+    rows = slice(0, 128) if mixed else half(1 - own)
+    for a, b in ((0, 32), (32, 64), (64, 96)):
+        t = jump(ready, T.yo, 16 * a, sw[n], T.ol, a, b)
+        need("y", *t)
+        sync.dma_start(T.y[rows, 16 * a:16 * b], T.yo[rows, 16 * a:16 * b]).then_inc(S.st, 16)
+        stored += 16
+    g.wait_ge(S.ls, sent)
+    need("y", ("st", stored), *[("c" + q, cnt[q]) for q in cnt])

@@ -5,12 +5,12 @@ N, P, NT, W = 6, 1536, 192, 768
 H = NT + W
 C = NT // 16
 LW = W // 16
+B = P // 3
 SCRATCH = {
     "lnb": ("sbuf", [128, C], "int32"), "dsb": ("sbuf", [128, C], "int32"),
-    "n1": ("sbuf", [128, C], "float32"), "sc": ("sbuf", [128, C], "float32"), "sch": ("sbuf", [128, 1], "float16"),
-    "ex": ("sbuf", [128, C], "float32"), "zi": ("sbuf", [128, C], "float32"), "zc": ("sbuf", [128, C], "float32"),
-    "zd": ("sbuf", [128, C], "float32"), "u": ("sbuf", [128, C], "float32"), "pre": ("sbuf", [128, C], "float32"),
-    "rs": ("sbuf", [128, 1], "float32"),
+    "n1": ("sbuf", [128, C], "float32"), "sc": ("sbuf", [128, C + 1], "float32"), "sch": ("sbuf", [128, 1], "float16"),
+    "zi": ("sbuf", [128, C], "float32"), "zc": ("sbuf", [128, C], "float32"),
+    "zd": ("sbuf", [128, C], "float32"), "pre": ("sbuf", [128, C], "float32"), "rs": ("sbuf", [128, 1], "float32"),
     "lasts": ("sbuf", [128, C], "uint16"), "firsts": ("sbuf", [128, C], "uint16"), "ci": ("sbuf", [128, C], "int32"),
     "cl": ("sbuf", [128, C], "uint16"),
     "pi": ("sbuf", [128, 1], "int32"), "pj": ("sbuf", [128, 1], "int32"), "pm": ("sbuf", [128, 1], "float32"),
@@ -33,7 +33,8 @@ SCRATCH = {
 }
 for _k in range(N):
     SCRATCH["sw%d" % _k] = ("sbuf", [128, H], "bfloat16")
-SEMAPHORES = ["cg", "cv", "cs", "cp", "dl", "dd", "dle", "lo", "lw", "st", "ls"] + ["ar%d" % k for k in range(N)] + ["la%d" % k for k in range(N)]
+SEMAPHORES = ["cg", "cv", "cs", "cp", "dl", "dd", "dle", "lo", "lw", "lz", "st", "ls"]
+SEMAPHORES += ["ar%d" % k for k in range(N)] + ["la%d" % k for k in range(N)]
 
 
 def rank_program(g, core, T, topo):
@@ -85,14 +86,22 @@ def rank_program(g, core, T, topo):
     qi = op("g", [], lambda: g.iota(T.qi[:], [[0, C], [1, 16]], 0, 0, **flag))
     zi = op("g", [], lambda: g.iota(T.zi[:], [[-1, C]], 1, 0, **flag))
     ci = op("g", [], lambda: g.iota(T.ci[:], [[1, C]], 0, 0))
+    idi = op("g", [], lambda: g.iota(T.idi[:], [[16, LW]], NT, 0)) if mixed else None
     b0 = op("g", [ones], lambda: g.affine_select(T.b0[:], T.ones[:, 0:128], [[-16, 8], [0, 16]], A.is_ge, 0.0, 0, 1))
     bo = op("g", [b0], lambda: g.affine_select(T.bo[:], T.b0[:], [[16, 8], [0, 16]], A.is_ge, 0.0, 15, -1))
     tri = op("g", [bo], lambda: g.affine_select(T.tri[:], T.bo[:], [[1, 128]], A.is_gt, 0.0, 0, -1))
     lt = op("g", [], lambda: g.iota(T.lt[:], [[1, C], [C, 16]], -H, 0, **flag))
     fi = op("g", [ones], lambda: g.affine_select(T.fi[:], T.ones[:], [[-1, 144]], A.is_equal, 0.0, 16, 1))
-    ia = op("g", [], lambda: g.iota(T.wa[:, 0:H], [[1, H]], -H, 0, **flag))
-    if mixed:
-        idi = op("g", [], lambda: g.iota(T.idi[:], [[16, LW]], NT, 0))
+    xg = op("g", [], lambda: g.iota(T.x[:, 1408:P], [[0, P - 1408]], 1, 0, **flag))
+    h2 = H // 2
+    ia = [op("g", [], lambda: g.iota(T.wa[:, a:a + h2], [[1, h2]], a - H, 0, **flag)) for a in (0, h2)]
+    blank = [(k, side) for k in range(n) for side in range(2) if stage[k][side] is None]
+    zero = blank if mixed else blank[1:]
+    need("y", zb)
+    sync.dma_start(sw[0][:, NT:H], T.yo[:, 0:W]).then_inc(S.lz, 16)
+    for k, side in zero:
+        sync.dma_start(sw[k][half(side), 0:NT], T.yo[half(side), 0:NT]).then_inc(S.lz, 16)
+    z0 = ("lz", 16 + 16 * len(zero) + (16 * len(blank) if mixed else 0))
     m0 = op("s", [zb], lambda: s.activation(T.m[:, 0:W], T.yo[:, 0:W], CP, bias=4096.0))
     m1 = op("s", [], lambda: s.activation(T.m[:, W:P], T.yo[:, 0:W], CP, bias=4096.0))
     pj = op("v", [pi], lambda: v.tensor_scalar(T.pj[:], T.pi[:], 15, None, A.bitwise_and))
@@ -104,90 +113,35 @@ def rank_program(g, core, T, topo):
     ml = op("v", [qi, pm], lambda: v.tensor_scalar(T.ml[:], T.qi[:], T.pm[:], None, A.is_gt))
     zc = op("v", [zi, p12], lambda: v.tensor_scalar(T.zc[:], T.zi[:], T.p12[:], None, A.add))
     mk = op("v", [qi], lambda: v.tensor_scalar(T.mk[:], T.qi[:], T.pm[:], None, A.is_equal))
-    x0 = op("v", [], lambda: v.memset(T.x[:, 0:W], 1.0))
+    s0 = op("v", [], lambda: v.memset(T.sc[:, 0:1], 0.0))
+    if mixed:
+        need("y", op("v", [idi, pm], lambda: v.tensor_scalar(T.idl[:], T.idi[:], T.pm[:], None, A.add)))
+        for k, side in blank:
+            sync.dma_start(T.cl5[half(side), LW * k:LW * k + LW], T.idl[half(side), :]).then_inc(S.lz, 16)
+    x0 = op("v", [], lambda: v.memset(T.x[:, 0:384], 1.0))
+    x1 = op("s", [], lambda: s.activation(T.x[:, 384:640], T.yo[:, 0:256], CP, bias=1.0))
 
     n1 = op("v", [("dl", 16)], lambda: v.tensor_scalar(T.n1[:], T.lnb[:], 1.0, None, A.add))
     zd = op("v", [zc, ("dd", 16)], lambda: v.tensor_tensor(T.zd[:], T.zc[:], T.dsb[:], A.subtract))
-    sc = op("v", [n1], lambda: v.tensor_tensor_scan(T.sc[:], T.n1[:], T.n1[:], 0.0, A.add, A.max))
-    u = op("v", [zd, n1], lambda: v.tensor_tensor(T.u[:], T.zd[:], T.n1[:], A.subtract))
-    pre = op("v", [sc, u], lambda: v.tensor_tensor(T.pre[:], T.u[:], T.sc[:], A.add))
-    ex = op("v", [sc], lambda: v.tensor_tensor(T.ex[:], T.sc[:], T.n1[:], A.subtract))
+    sc = op("v", [n1, s0], lambda: v.tensor_tensor_scan(T.sc[:, 1:C + 1], T.n1[:], T.n1[:], 0.0, A.add, A.max))
+    pre = op("v", [sc, zd], lambda: v.tensor_tensor(T.pre[:], T.sc[:, 0:C], T.zd[:], A.add))
     gm = op("v", [pre, cl, mk], lambda: v.tensor_tensor(T.gm[:], T.pre[:, 0:C].indirect(T.cl[:, 0:C]), T.mk[:], A.mult))
-    sch = op("s", [sc], lambda: s.activation(T.sch[:], T.sc[:, C - 1:C], CP))
-    yt = op("s", [sc, ml], lambda: s.activation(T.yt[:], T.ml[:], CP, scale=T.sc[:, C - 1:C]))
-    x1 = op("s", [x0], lambda: s.activation(T.x[:, W:P], T.x[:, 0:W], CP))
+    sch = op("s", [sc], lambda: s.activation(T.sch[:], T.sc[:, C:C + 1], CP))
+    yt = op("s", [sc, ml], lambda: s.activation(T.yt[:], T.ml[:], CP, scale=T.sc[:, C:C + 1]))
+    x2 = op("s", [], lambda: s.activation(T.x[:, 640:1408], T.yo[:, 0:W], CP, bias=1.0))
     op("p", [bo, c60], lambda: pe.matmul(T.rep[:, 0:NT], T.bo[:], T.c60[:], True, False))
     car = op("p", [tri, sch], lambda: pe.matmul(T.car[:, 0:1], T.tri[:], T.sch[:], True, True))
     op("p", [yt], lambda: pe.matmul(T.rep[:, 0:NT], T.bo[:], T.yt[:], False, False))
     rep = op("p", [gm], lambda: pe.matmul(T.rep[:, 0:NT], T.bo[:], T.gm[:], False, True))
-    lasts = op("v", [car, sc], lambda: v.tensor_scalar(T.lasts[:], T.sc[:], T.car[:, 0:1], -1.0, A.add, A.add))
-    firsts = op("v", [car, ex], lambda: v.tensor_scalar(T.firsts[:], T.ex[:], T.car[:, 0:1], None, A.add))
+    lasts = op("v", [car, sc], lambda: v.tensor_scalar(T.lasts[:], T.sc[:, 1:C + 1], T.car[:, 0:1], -1.0, A.add, A.add))
+    firsts = op("v", [car, sc], lambda: v.tensor_scalar(T.firsts[:], T.sc[:, 0:C], T.car[:, 0:1], None, A.add))
     ms = op("v", [lasts, lt, m0, m1], lambda: v.tensor_copy(T.m[:, 0:P].indirect(T.lasts[:, 0:C]), T.lt[:]))
     xd = op("s", [rep], lambda: s.activation(T.xd[:], T.rep[:, 0:NT], CP))
-    f = op("v", [f0, fi], lambda: v.tensor_scalar(T.f[:], T.fi[:], T.p0[:], None, A.mult))
-    xs = op("v", [firsts, xd, x1], lambda: v.tensor_copy(T.x[:, 0:P].indirect(T.firsts[:, 0:C]), T.xd[:]))
-    B = P // 3
+    f = op("s", [f0, fi], lambda: s.activation(T.f[:], T.fi[:], CP, scale=T.p0[:]))
+    xs = op("v", [firsts, xd, x0, x1, x2, xg], lambda: v.tensor_copy(T.x[:, 0:P].indirect(T.firsts[:, 0:C]), T.xd[:]))
     ra = op("v", [ms, xs], lambda: v.tensor_tensor_scan(T.r[:, 0:B], T.x[:, 0:B], T.m[:, 0:B], -float(H + 1), A.add, A.min))
     rs = op("v", [ra], lambda: v.tensor_copy(T.rs[:], T.r[:, B - 1:B]))
     rb = op("v", [rs], lambda: v.tensor_tensor_scan(T.r[:, B:P], T.x[:, B:P], T.m[:, B:P], T.rs[:], A.add, A.min))
-    ib = op("s", [ia], lambda: s.activation(T.wb[:, 0:H], T.wa[:, 0:H], CP))
-
-    def conv(deps, out, a, b):
-        need("p", *deps)
-        for q in range(16):
-            t = op("p", [], lambda: pe.matmul(out[:, a // 16:b // 16], T.f[:, 16 - q:144 - q], T.r[:, a + q:b:16], q == 0, q == 15))
-        return t
-
-    def emit(dep, out, a, b, src):
-        return op("v", [dep], lambda: v.tensor_scalar(out[:, a:b], src[:, a:b], float(H), None, A.add))
-
-    def jump(deps, out, o, win, lst, a, b):
-        h = (a + b) // 2
-        e = o + 16 * (h - a)
-        z = win.shape[1]
-        t1 = op("v", deps, lambda: v.tensor_copy(out[:, o:e], win[:, 0:z].indirect(lst[:, a:h])))
-        t2 = op("s", deps, lambda: s.activation(out[:, e:o + 16 * (b - a)], win[:, 0:z].indirect(lst[:, h:b]), CP))
-        return [t1, t2]
-
-    full = P // 16
-    win, oth, lst, nxt = T.wa, T.wb, T.la, T.lb
-    conv([ra, f], T.cva, 0, B)
-    cp = conv([rb], T.cva, B, P)
-    ready = [op("s", [rb], lambda: s.activation(win[:, H + W:H + P], T.r[:, W:P], CP)),
-             op("v", [rb], lambda: v.tensor_copy(win[:, H:H + W], T.r[:, 0:W])), ia, ib]
-    z0 = op("v", [], lambda: v.memset(sw[0][:, NT:H], 0.0))
-    for k in range(n):
-        if None in stage[k] and (k or mixed):
-            z0 = op("v", [], lambda: v.memset(sw[k][half(stage[k].index(None)), 0:NT], 0.0))
-    if mixed:
-        idl = op("v", [idi], lambda: v.tensor_scalar(T.idl[:], T.idi[:], T.pm[:], None, A.add))
-        for k in range(n):
-            for side in range(2):
-                if stage[k][side] is None:
-                    z0 = op("v", [idl], lambda: v.tensor_copy(T.cl5[half(side), LW * k:LW * k + LW], T.idl[half(side), :]))
-    ready.append(emit(cp, lst, 0, full, T.cva))
-    for extra in (1, 1, 2):
-        t = jump(ready, T.r, 0, win, lst, 0, full)
-        cp = conv(t, T.cva, 0, P)
-        ready = [op("v", t[:1], lambda: v.tensor_copy(oth[:, H:H + W], T.r[:, 0:W])),
-                 op("s", t[1:], lambda: s.activation(oth[:, H + W:H + P], T.r[:, W:P], CP))]
-        win, oth = oth, win
-        for _ in range(extra):
-            ready = jump(ready, oth, H, win, lst, 0, full)
-            win, oth = oth, win
-        ready.append(emit(cp, nxt, 0, full, T.cva))
-        lst, nxt = nxt, lst
-    t = jump(ready, T.r, W, win, lst, LW, full)
-    cp = conv(t, T.cva, W, P)
-    t = jump(ready, T.r, 0, win, lst, 0, LW)
-    cq = conv(t, T.cvb, 0, W)
-    tail = emit(cp, T.ol, LW, full, T.cva)
-    te = []
-    if not mixed:
-        te += jump([tail, z0, ("lo", 32), ("lw", 16 * (up + down))], T.ye, W, sw[0], T.ol, LW, full)
-    head = emit(cq, T.ol, 0, LW, T.cvb)
-    if not mixed:
-        te += jump([head], T.ye, 0, sw[0], T.ol, 0, LW)
 
     def ids(rs):
         out = []
@@ -219,12 +173,76 @@ def rank_program(g, core, T, topo):
     g.wait_ge(S.dle, 16)
     g.remote_dma_fused(trs, local_sem=S.ls)
     sent = sum(len(e) for e in letter_engines(rank))
+
+    def conv(deps, out, a, b):
+        need("p", *deps)
+        for q in range(16):
+            t = op("p", [], lambda: pe.matmul(out[:, a // 16:b // 16], T.f[:, 16 - q:144 - q], T.r[:, a + q:b:16], q == 0, q == 15))
+        return t
+
+    def emit(dep, out, a, b, src):
+        return op("v", [dep], lambda: v.tensor_scalar(out[:, a:b], src[:, a:b], float(H), None, A.add))
+
+    def jump(deps, out, o, win, lst, a, b):
+        h = (a + b) // 2
+        e = o + 16 * (h - a)
+        z = win.shape[1]
+        t1 = op("v", deps, lambda: v.tensor_copy(out[:, o:e], win[:, 0:z].indirect(lst[:, a:h])))
+        t2 = op("s", deps, lambda: s.activation(out[:, e:o + 16 * (b - a)], win[:, 0:z].indirect(lst[:, h:b]), CP))
+        return [t1, t2]
+
+    def widen(q, dep, out, a, b):
+        if q == "g":
+            return op(q, dep, lambda: g.affine_select(out[:, H + a:H + b], T.r[:, a:b], [[0, b - a]], A.is_equal, 0.0, 0, 0))
+        if q == "s":
+            return op(q, dep, lambda: s.activation(out[:, H + a:H + b], T.r[:, a:b], CP))
+        return op(q, dep, lambda: v.tensor_copy(out[:, H + a:H + b], T.r[:, a:b]))
+
+    full, BC, w2, kb = P // 16, B // 16, W // 2, (B + P) // 2
+    win, oth, lst, nxt = T.wa, T.wb, T.la, T.lb
+    c1, c2 = conv([ra, f], T.cva, 0, B), conv([rb], T.cvb, B, P)
+    op("s", ia[:1], lambda: s.activation(T.wb[:, 0:h2], T.wa[:, 0:h2], CP))
+    ka = widen("s", [ra], win, 0, B)
+    ib = op("s", ia[1:], lambda: s.activation(T.wb[:, h2:H], T.wa[:, h2:H], CP))
+    ready = [ka, widen("v", [rb], win, B, kb), widen("s", [rb], win, kb, P)] + ia
+    cols = ((0, BC), (BC, full))
+    first = (cols, (("g", 0, 0, B), ("v", 1, B, kb), ("s", 1, kb, P)), 1)
+    later = (((LW, full), (0, LW)), (("g", 0, W, W + 512), ("v", 1, 0, w2), ("s", 1, w2, W), ("s", 0, W + 512, W + 640), ("v", 0, W + 640, P)), 0)
+    for (a, b), spec, extra in (first, later, later, later):
+        e1 = emit(c1, lst, cols[0][0], cols[0][1], T.cva)
+        t1 = jump(ready + [e1], T.r, 16 * a[0], win, lst, a[0], a[1]) if a == cols[0] else None
+        e2 = emit(c2, lst, cols[1][0], cols[1][1], T.cvb)
+        if t1 is None:
+            t1 = jump(ready + [e1, e2], T.r, 16 * a[0], win, lst, a[0], a[1])
+        c1 = conv(t1, T.cva, 16 * a[0], 16 * a[1])
+        t2 = jump([e2], T.r, 16 * b[0], win, lst, b[0], b[1])
+        c2 = conv(t2, T.cvb, 16 * b[0], 16 * b[1])
+        ready = [widen(q, (t1, t2)[w], oth, x, z) for q, w, x, z in spec] + [ib]
+        win, oth = oth, win
+        for _ in range(extra):
+            ready = jump(ready, oth, H, win, lst, 0, full)
+            win, oth = oth, win
+        lst, nxt = nxt, lst
+        cols = (a, b)
+    e1 = emit(c1, lst, cols[0][0], cols[0][1], T.cva)
+    t = jump(ready + [e1], T.r, W, win, lst, LW, full)
+    cp = conv(t, T.cva, W, P)
+    e2 = emit(c2, lst, cols[1][0], cols[1][1], T.cvb)
+    t = jump([e2], T.r, 0, win, lst, 0, LW)
+    cq = conv(t, T.cvb, 0, W)
+    tail = emit(cp, T.ol, LW, full, T.cva)
+    te = []
+    if not mixed:
+        te += jump([tail, z0, ("lo", 32), ("lw", 16 * (up + down))], T.ye, W, sw[0], T.ol, LW, full)
+    head = emit(cq, T.ol, 0, LW, T.cvb)
+    if not mixed:
+        te += jump([head], T.ye, 0, sw[0], T.ol, 0, LW)
+
     need("g", tail)
     g.remote_dma_fused([RemoteDMATransfer(dst_ids=ids(others), dma_engine_mask=bits(shared(rank)), remote_sem=S["ar%d" % rank],
                                           srcs=[T.ol[:, LW:full]], dsts=[T.ll[:, LW * rank:LW * rank + LW] for _ in others])], local_sem=S.ls)
     sent += len(shared(rank))
 
-    need("y", z0)
     for k in range(n):
         for side in range(2):
             src = stage[k][side]

@@ -6,29 +6,32 @@ H = NT + W
 C = NT // 16
 LW = W // 16
 B = P // 3
+K = 256
+CT, LT, TT, IA, IB = 0, 4, 7, 8, 9
 SCRATCH = {
-    "lnb": ("sbuf", [128, C], "int32"), "dsb": ("sbuf", [128, C], "int32"),
-    "n1": ("sbuf", [128, C], "float32"), "sc": ("sbuf", [128, C + 1], "float32"), "sch": ("sbuf", [128, 1], "float16"),
-    "zi": ("sbuf", [128, C], "float32"), "zc": ("sbuf", [128, C], "float32"),
-    "zd": ("sbuf", [128, C], "float32"), "pre": ("sbuf", [128, C], "float32"), "rs": ("sbuf", [128, 1], "float32"),
-    "lasts": ("sbuf", [128, C], "uint16"), "firsts": ("sbuf", [128, C], "uint16"), "ci": ("sbuf", [128, C], "int32"),
-    "cl": ("sbuf", [128, C], "uint16"),
-    "pi": ("sbuf", [128, 1], "int32"), "pj": ("sbuf", [128, 1], "int32"), "pm": ("sbuf", [128, 1], "float32"),
-    "p12": ("sbuf", [128, 1], "float32"), "p0": ("sbuf", [128, 1], "float32"),
-    "qi": ("sbuf", [128, NT], "float32"), "mk": ("sbuf", [128, NT], "float16"), "ml": ("sbuf", [128, NT], "float16"),
-    "c60": ("sbuf", [128, NT], "float16"), "yt": ("sbuf", [128, NT], "float16"), "gm": ("sbuf", [128, NT], "float16"),
-    "lt": ("sbuf", [128, NT], "float32"), "xd": ("sbuf", [128, NT], "float32"),
-    "ones": ("sbuf", [128, 144], "float16"), "fi": ("sbuf", [128, 144], "float16"), "f": ("sbuf", [128, 144], "float16"),
-    "b0": ("sbuf", [128, 128], "float16"), "bo": ("sbuf", [128, 128], "float16"), "tri": ("sbuf", [128, 128], "float16"),
-    "m": ("sbuf", [128, P], "float32"), "x": ("sbuf", [128, P], "float32"),
-    "r": ("sbuf", [128, P], "float16"),
-    "wa": ("sbuf", [128, H + P], "float32"), "wb": ("sbuf", [128, H + P], "float32"),
+    "lnb": ("sbuf", [128, C], "int32"), "dsr": ("sbuf", [128, NT], "int32"),
+    "sc": ("sbuf", [128, C], "float32"), "sch": ("sbuf", [128, 1], "float16"),
+    "lasts": ("sbuf", [128, C], "uint16"), "ci": ("sbuf", [128, C + 1], "int32"), "cl": ("sbuf", [128, C + 2], "uint16"),
+    "pi": ("sbuf", [128, 1], "int32"), "pj": ("sbuf", [128, 1], "int32"), "pf": ("sbuf", [128, 1], "float32"),
+    "cut": ("sbuf", [128, 1], "float32"), "p12": ("sbuf", [128, 1], "float32"), "pm": ("sbuf", [128, 1], "float32"),
+    "mc": ("sbuf", [128, 1], "float32"), "mt": ("sbuf", [128, 1], "float32"),
+    "ma": ("sbuf", [128, 1], "float32"), "mb": ("sbuf", [128, 1], "float32"),
+    "ck": ("sbuf", [128, 10], "float32"), "cb": ("sbuf", [128, 10], "float32"),
+    "ones": ("sbuf", [128, K], "bfloat16"), "cnt": ("sbuf", [128, K], "bfloat16"),
+    "e0": ("sbuf", [128, 132], "float16"), "e1": ("sbuf", [128, 132], "float16"),
+    "qp": ("sbuf", [128, 132], "float16"), "qn": ("sbuf", [128, 132], "float16"),
+    "gt": ("sbuf", [128, 128], "float16"), "tri": ("sbuf", [128, 128], "float16"),
+    "f0": ("sbuf", [128, 144], "bfloat16"), "f1": ("sbuf", [128, 144], "bfloat16"), "f": ("sbuf", [128, 144], "bfloat16"),
+    "lt": ("sbuf", [128, NT], "bfloat16"), "ct": ("sbuf", [128, NT], "bfloat16"),
+    "rd": ("sbuf", [128, NT + 16], "float16"), "z": ("sbuf", [128, NT], "bfloat16"),
+    "d0": ("sbuf", [128, B], "bfloat16"), "d1": ("sbuf", [128, P], "bfloat16"),
+    "wa": ("sbuf", [128, H + P], "bfloat16"), "wb": ("sbuf", [128, H + P], "bfloat16"),
     "la": ("sbuf", [128, P // 16], "uint16"), "lb": ("sbuf", [128, P // 16], "uint16"), "ol": ("sbuf", [128, P // 16], "uint16"),
     "idi": ("sbuf", [128, LW], "int32"), "idl": ("sbuf", [128, LW], "uint16"),
     "ll": ("sbuf", [128, N * LW], "uint16"), "cl5": ("sbuf", [128, N * LW], "uint16"),
     "yo": ("sbuf", [128, P], "bfloat16"), "ye": ("sbuf", [128, P], "bfloat16"),
     "dle": ("dram", [2, 128, NT // 2], "bfloat16"), "lel": ("dram", [N, 128, NT // 2], "bfloat16"),
-    "car": ("psum", [128, 512], "float32"), "rep": ("psum", [128, 512], "float32"),
+    "car": ("psum", [128, 512], "float32"), "zp": ("psum", [128, 512], "float32"), "ini": ("psum", [128, 512], "float32"),
     "cva": ("psum", [128, 512], "float32"), "cvb": ("psum", [128, 512], "float32"),
 }
 for _k in range(N):
@@ -41,7 +44,7 @@ def rank_program(g, core, T, topo):
     rank = T.rank_of(core)
     if rank is None:
         return
-    A, CP = AluOpType, ActivationFunctionType.Copy
+    A, CP, ID = AluOpType, ActivationFunctionType.Copy, ActivationFunctionType.Identity
     v, s, pe, sync, S = g.vector, g.scalar, g.tensor, g.sync, T.sem
     queue = {"g": g, "v": v, "s": s, "p": pe, "y": sync}
     cnt = {"g": 0, "v": 0, "s": 0, "p": 0}
@@ -59,6 +62,9 @@ def rank_program(g, core, T, topo):
         ins().then_inc(S["c" + q], 1)
         return ("c" + q, cnt[q])
 
+    def ts(out, in0, s1, s2, *ops):
+        return lambda: v.tensor_scalar(out, in0, s1, s2, *ops)
+
     up, down = rank, N - 1 - rank
     n = max(up, down)
     mixed = up > 0 and down > 0
@@ -73,75 +79,78 @@ def rank_program(g, core, T, topo):
         return slice(64 * side, 64 * side + 64)
 
     sync.dma_start(T.lnb[:], T.ln[:]).then_inc(S.dl, 16)
-    s.dma_start(T.dsb[:], T.ds[:]).then_inc(S.dd, 16)
+    dz = op("v", [], lambda: v.memset(T.dsr[:], 0))
+    need("y", dz)
+    need("s", dz)
+    sync.dma_start(T.dsr[CT:128:16, :], T.ds[:]).then_inc(S.dd, 16)
+    s.dma_start(T.dsr[CT + 1:128:16, :], T.ds[:]).then_inc(S.dd, 16)
+    sync.dma_start(T.dsr[CT + 2:128:16, :], T.ds[:]).then_inc(S.dd, 16)
     sync.dma_start(T.dle[:], T.le[:]).then_inc(S.dle, 16)
     sync.dma_start(sw[n][:, 0:NT], T.le[:]).then_inc(S.lo, 16)
     if not mixed:
         sync.dma_start(sw[0][half(own), 0:NT], T.le[half(own), :]).then_inc(S.lo, 16)
 
     flag = {"allow_small_or_imprecise_dtypes": True}
-    ones = op("v", [], lambda: v.memset(T.ones[:], 1.0))
     pi = op("g", [], lambda: g.iota(T.pi[:], [[1, 1]], 0, 1))
-    zb = op("v", [], lambda: v.memset(T.yo[:, 0:W], 0.0))
-    qi = op("g", [], lambda: g.iota(T.qi[:], [[0, C], [1, 16]], 0, 0, **flag))
-    zi = op("g", [], lambda: g.iota(T.zi[:], [[-1, C]], 1, 0, **flag))
-    ci = op("g", [], lambda: g.iota(T.ci[:], [[1, C]], 0, 0))
+    ci = op("g", [], lambda: g.iota(T.ci[:], [[1, C + 1]], 0, 0))
+    pf = op("g", [], lambda: g.iota(T.pf[:], [[1, 1]], 0, 1, **flag))
+    ck = op("g", [], lambda: g.iota(T.ck[:], [[K, 10]], 0, 0, **flag))
+    lt = op("g", [], lambda: g.iota(T.lt[:], [[1, C], [C, 16]], 0, 0, **flag))
+    ones = op("v", [], lambda: v.memset(T.ones[:], 1.0))
+    pj = op("v", [pi], ts(T.pj[:], T.pi[:], 15, None, A.bitwise_and))
+    co = op("v", [ones], lambda: v.tensor_tensor_scan(T.cnt[:], T.ones[:], T.ones[:], -1.0, A.add, A.mult))
+    mc = op("v", [pj], ts(T.mc[:], T.pj[:], float(CT + 3), None, A.is_lt))
+    p12 = op("v", [], ts(T.p12[:], T.pj[:], float(C), None, A.mult))
+    cut = op("v", [], ts(T.cut[:], T.pj[:], -float(K), None, A.mult))
+    gt = op("v", [co, pf], ts(T.gt[:], T.cnt[:, 0:128], T.pf[:], None, A.is_gt))
+    cl = op("v", [p12, ci], ts(T.cl[:, 0:C + 1], T.ci[:], T.p12[:], float(NT - 1), A.add, A.min))
+    op("v", [], ts(T.e0[:], T.cnt[:, 0:132], T.pf[:], float(LT), A.subtract, A.is_equal))
+    e1 = op("v", [], ts(T.e1[:], T.cnt[:, 0:132], T.pf[:], float(LT - 1), A.subtract, A.is_equal))
+    ma = op("v", [], ts(T.ma[:], T.pj[:], float(IA), None, A.is_equal))
+    mb = op("v", [], ts(T.mb[:], T.pj[:], float(IB), None, A.is_equal))
+    qp = op("v", [e1], lambda: v.tensor_tensor(T.qp[:], T.e0[:], T.e1[:], A.subtract))
+    cb = op("v", [mb, ck], ts(T.cb[:], T.ck[:], T.mb[:], None, A.mult))
+    qn = op("v", [qp], ts(T.qn[:], T.qp[:], -1.0, None, A.mult))
+    mt = op("v", [], ts(T.mt[:], T.pj[:], float(TT), None, A.is_equal))
+    tri = op("g", [gt], lambda: g.affine_select(T.tri[:], T.gt[:], [[-16, 8], [0, 16]], A.is_ge, 0.0, 0, 1))
+    f0 = op("g", [ones], lambda: g.affine_select(T.f0[:], T.ones[:, 0:144], [[-16, 9], [-4096, 16]], A.is_ge, 0.0, 16, 1))
+    f1 = op("g", [f0], lambda: g.affine_select(T.f1[:], T.f0[:], [[16, 9], [-4096, 16]], A.is_ge, 0.0, 14 - 16, -1))
+    f = op("g", [f1], lambda: g.affine_select(T.f[:], T.f1[:], [[-16, 9], [0, 16]], A.not_equal, 0.0, 16 - (CT + 3), 1))
     idi = op("g", [], lambda: g.iota(T.idi[:], [[16, LW]], NT, 0)) if mixed else None
-    b0 = op("g", [ones], lambda: g.affine_select(T.b0[:], T.ones[:, 0:128], [[-16, 8], [0, 16]], A.is_ge, 0.0, 0, 1))
-    bo = op("g", [b0], lambda: g.affine_select(T.bo[:], T.b0[:], [[16, 8], [0, 16]], A.is_ge, 0.0, 15, -1))
-    tri = op("g", [bo], lambda: g.affine_select(T.tri[:], T.bo[:], [[1, 128]], A.is_gt, 0.0, 0, -1))
-    lt = op("g", [], lambda: g.iota(T.lt[:], [[1, C], [C, 16]], -H, 0, **flag))
-    fi = op("g", [ones], lambda: g.affine_select(T.fi[:], T.ones[:], [[-1, 144]], A.is_equal, 0.0, 16, 1))
-    xg = op("g", [], lambda: g.iota(T.x[:, 1408:P], [[0, P - 1408]], 1, 0, **flag))
-    h2 = H // 2
-    ia = [op("g", [], lambda: g.iota(T.wa[:, a:a + h2], [[1, h2]], a - H, 0, **flag)) for a in (0, h2)]
-    blank = [(k, side) for k in range(n) for side in range(2) if stage[k][side] is None]
-    zero = blank if mixed else blank[1:]
-    need("y", zb)
-    sync.dma_start(sw[0][:, NT:H], T.yo[:, 0:W]).then_inc(S.lz, 16)
-    for k, side in zero:
-        sync.dma_start(sw[k][half(side), 0:NT], T.yo[half(side), 0:NT]).then_inc(S.lz, 16)
-    z0 = ("lz", 16 + 16 * len(zero) + (16 * len(blank) if mixed else 0))
-    m0 = op("s", [zb], lambda: s.activation(T.m[:, 0:W], T.yo[:, 0:W], CP, bias=4096.0))
-    m1 = op("s", [], lambda: s.activation(T.m[:, W:P], T.yo[:, 0:W], CP, bias=4096.0))
-    pj = op("v", [pi], lambda: v.tensor_scalar(T.pj[:], T.pi[:], 15, None, A.bitwise_and))
-    c60 = op("v", [], lambda: v.memset(T.c60[:], 60.0))
-    pm = op("v", [pj], lambda: v.tensor_copy(T.pm[:], T.pj[:]))
-    cl = op("v", [ci], lambda: v.tensor_copy(T.cl[:], T.ci[:]))
-    p12 = op("v", [pm], lambda: v.tensor_scalar(T.p12[:], T.pm[:], -float(C), None, A.mult))
-    f0 = op("v", [pm], lambda: v.tensor_scalar(T.p0[:], T.pm[:], 0.0, None, A.is_equal))
-    ml = op("v", [qi, pm], lambda: v.tensor_scalar(T.ml[:], T.qi[:], T.pm[:], None, A.is_gt))
-    zc = op("v", [zi, p12], lambda: v.tensor_scalar(T.zc[:], T.zi[:], T.p12[:], None, A.add))
-    mk = op("v", [qi], lambda: v.tensor_scalar(T.mk[:], T.qi[:], T.pm[:], None, A.is_equal))
-    s0 = op("v", [], lambda: v.memset(T.sc[:, 0:1], 0.0))
-    if mixed:
-        need("y", op("v", [idi, pm], lambda: v.tensor_scalar(T.idl[:], T.idi[:], T.pm[:], None, A.add)))
-        for k, side in blank:
-            sync.dma_start(T.cl5[half(side), LW * k:LW * k + LW], T.idl[half(side), :]).then_inc(S.lz, 16)
-    x0 = op("v", [], lambda: v.memset(T.x[:, 0:384], 1.0))
-    x1 = op("s", [], lambda: s.activation(T.x[:, 384:640], T.yo[:, 0:256], CP, bias=1.0))
 
-    n1 = op("v", [("dl", 16)], lambda: v.tensor_scalar(T.n1[:], T.lnb[:], 1.0, None, A.add))
-    zd = op("v", [zc, ("dd", 16)], lambda: v.tensor_tensor(T.zd[:], T.zc[:], T.dsb[:], A.subtract))
-    sc = op("v", [n1, s0], lambda: v.tensor_tensor_scan(T.sc[:, 1:C + 1], T.n1[:], T.n1[:], 0.0, A.add, A.max))
-    pre = op("v", [sc, zd], lambda: v.tensor_tensor(T.pre[:], T.sc[:, 0:C], T.zd[:], A.add))
-    gm = op("v", [pre, cl, mk], lambda: v.tensor_tensor(T.gm[:], T.pre[:, 0:C].indirect(T.cl[:, 0:C]), T.mk[:], A.mult))
-    sch = op("s", [sc], lambda: s.activation(T.sch[:], T.sc[:, C:C + 1], CP))
-    yt = op("s", [sc, ml], lambda: s.activation(T.yt[:], T.ml[:], CP, scale=T.sc[:, C:C + 1]))
-    x2 = op("s", [], lambda: s.activation(T.x[:, 640:1408], T.yo[:, 0:W], CP, bias=1.0))
-    op("p", [bo, c60], lambda: pe.matmul(T.rep[:, 0:NT], T.bo[:], T.c60[:], True, False))
+    def columns(q, deps, out, o, a, b):
+        while a < b:
+            k, e = a // K, min(b, (a // K + 1) * K)
+            src = T.cnt[:, a - K * k:e - K * k]
+            if q == "v":
+                t = op(q, deps, ts(out[:, o:o + e - a], src, T.ma[:], T.cb[:, k:k + 1], A.mult, A.add))
+            else:
+                t = op(q, deps, lambda: s.activation(out[:, o:o + e - a], src, ID, T.cb[:, k:k + 1], T.ma[:]))
+            o, a = o + e - a, e
+        return t
+
+    dc = [op("s", [mc, ones], lambda: s.activation(T.d0[:, x:x + K], T.ones[:], CP, scale=T.mc[:])) for x in (0, K)][-1]
+    x1 = columns("s", [co, ma, cb], T.d1, 1280 - H, 1280, 2048)
+    sc = op("v", [("dl", 16), ones], lambda: v.tensor_tensor_scan(T.sc[:], T.lnb[:], T.ones[:, 0:C], 0.0, A.add, A.add))
+    rd = op("v", [cl, cut, ("dd", 48)], ts(T.rd[:], T.dsr[:, 0:NT].indirect(T.cl[:, 0:C + 1]), T.cut[:], 0.0, A.add, A.max))
+    sch = op("v", [sc], lambda: v.tensor_copy(T.sch[:], T.sc[:, C - 1:C]))
     car = op("p", [tri, sch], lambda: pe.matmul(T.car[:, 0:1], T.tri[:], T.sch[:], True, True))
-    op("p", [yt], lambda: pe.matmul(T.rep[:, 0:NT], T.bo[:], T.yt[:], False, False))
-    rep = op("p", [gm], lambda: pe.matmul(T.rep[:, 0:NT], T.bo[:], T.gm[:], False, True))
-    lasts = op("v", [car, sc], lambda: v.tensor_scalar(T.lasts[:], T.sc[:, 1:C + 1], T.car[:, 0:1], -1.0, A.add, A.add))
-    firsts = op("v", [car, sc], lambda: v.tensor_scalar(T.firsts[:], T.sc[:, 0:C], T.car[:, 0:1], None, A.add))
-    ms = op("v", [lasts, lt, m0, m1], lambda: v.tensor_copy(T.m[:, 0:P].indirect(T.lasts[:, 0:C]), T.lt[:]))
-    xd = op("s", [rep], lambda: s.activation(T.xd[:], T.rep[:, 0:NT], CP))
-    f = op("s", [f0, fi], lambda: s.activation(T.f[:], T.fi[:], CP, scale=T.p0[:]))
-    xs = op("v", [firsts, xd, x0, x1, x2, xg], lambda: v.tensor_copy(T.x[:, 0:P].indirect(T.firsts[:, 0:C]), T.xd[:]))
-    ra = op("v", [ms, xs], lambda: v.tensor_tensor_scan(T.r[:, 0:B], T.x[:, 0:B], T.m[:, 0:B], -float(H + 1), A.add, A.min))
-    rs = op("v", [ra], lambda: v.tensor_copy(T.rs[:], T.r[:, B - 1:B]))
-    rb = op("v", [rs], lambda: v.tensor_tensor_scan(T.r[:, B:P], T.x[:, B:P], T.m[:, B:P], T.rs[:], A.add, A.min))
+    ct = op("v", [lt, mt], ts(T.ct[:], T.lt[:], T.mt[:], None, A.mult))
+    columns("v", [cb], T.d1, 0, H, 1280)
+    lasts = op("v", [car, sc], ts(T.lasts[:], T.sc[:], T.car[:, 0:1], -1.0, A.add, A.add))
+    x0 = columns("v", [], T.d1, 2048 - H, 2048, H + P)
+    op("p", [qn, rd], lambda: pe.matmul(T.zp[:, 0:NT], T.qn[:, LT:LT + 128], T.rd[:, 16:NT + 16], True, False))
+    op("p", [], lambda: pe.matmul(T.zp[:, 0:NT], T.qp[:, LT:LT + 128], T.rd[:, 0:NT], False, False))
+    zp = op("p", [], lambda: pe.matmul(T.zp[:, 0:NT], T.qp[:, 0:128], T.rd[:, 16:NT + 16], False, True))
+    ini = op("p", [], lambda: pe.matmul(T.ini[:, 0:1], T.qn[:, LT:LT + 128], T.rd[:, 0:1], True, True))
+    z = op("v", [zp, ct], lambda: v.tensor_tensor(T.z[:], T.zp[:, 0:NT], T.ct[:], A.add))
+    zs = op("v", [z, lasts, x0, x1], lambda: v.tensor_copy(T.d1[:, 0:P].indirect(T.lasts[:, 0:C]), T.z[:]))
+    r = []
+    for a in range(0, P, B):
+        r.append(op("v", r[-1:] if r else [zs, dc, ini], lambda: v.tensor_tensor_scan(
+            T.wa[:, H + a:H + a + B], T.d0[:], T.d1[:, a:a + B], T.wa[:, H + a - 1:H + a] if a else T.ini[:, 0:1], A.mult, A.add)))
+    ia = [columns("v", [], T.wa, 0, 0, 2 * K), columns("s", [], T.wa, 2 * K, 2 * K, H)]
+    ib = columns("s", [], T.wb, 0, 0, H)
 
     def ids(rs):
         out = []
@@ -174,14 +183,27 @@ def rank_program(g, core, T, topo):
     g.remote_dma_fused(trs, local_sem=S.ls)
     sent = sum(len(e) for e in letter_engines(rank))
 
-    def conv(deps, out, a, b):
+    blank = [(k, side) for k in range(n) for side in range(2) if stage[k][side] is None]
+    zero = blank if mixed else blank[1:]
+    need("y", op("v", [], lambda: v.memset(T.yo[:, 0:W], 0.0)))
+    sync.dma_start(sw[0][:, NT:H], T.yo[:, 0:W]).then_inc(S.lz, 16)
+    for k, side in zero:
+        sync.dma_start(sw[k][half(side), 0:NT], T.yo[half(side), 0:NT]).then_inc(S.lz, 16)
+    z0 = ("lz", 16 + 16 * len(zero) + (16 * len(blank) if mixed else 0))
+    if mixed:
+        pm = op("v", [], lambda: v.tensor_copy(T.pm[:], T.pj[:]))
+        need("y", op("v", [idi, pm], ts(T.idl[:], T.idi[:], T.pm[:], None, A.add)))
+        for k, side in blank:
+            sync.dma_start(T.cl5[half(side), LW * k:LW * k + LW], T.idl[half(side), :]).then_inc(S.lz, 16)
+
+    def conv(deps, out, win, a, b):
         need("p", *deps)
         for q in range(16):
-            t = op("p", [], lambda: pe.matmul(out[:, a // 16:b // 16], T.f[:, 16 - q:144 - q], T.r[:, a + q:b:16], q == 0, q == 15))
+            t = op("p", [], lambda: pe.matmul(out[:, a // 16:b // 16], T.f[:, 16 - q:144 - q], win[:, H + a + q:H + b:16], q == 0, q == 15))
         return t
 
     def emit(dep, out, a, b, src):
-        return op("v", [dep], lambda: v.tensor_scalar(out[:, a:b], src[:, a:b], float(H), None, A.add))
+        return op("v", [dep], lambda: v.tensor_copy(out[:, a:b], src[:, a:b]))
 
     def jump(deps, out, o, win, lst, a, b):
         h = (a + b) // 2
@@ -191,45 +213,34 @@ def rank_program(g, core, T, topo):
         t2 = op("s", deps, lambda: s.activation(out[:, e:o + 16 * (b - a)], win[:, 0:z].indirect(lst[:, h:b]), CP))
         return [t1, t2]
 
-    def widen(q, dep, out, a, b):
-        if q == "g":
-            return op(q, dep, lambda: g.affine_select(out[:, H + a:H + b], T.r[:, a:b], [[0, b - a]], A.is_equal, 0.0, 0, 0))
-        if q == "s":
-            return op(q, dep, lambda: s.activation(out[:, H + a:H + b], T.r[:, a:b], CP))
-        return op(q, dep, lambda: v.tensor_copy(out[:, H + a:H + b], T.r[:, a:b]))
-
-    full, BC, w2, kb = P // 16, B // 16, W // 2, (B + P) // 2
+    full, BC = P // 16, B // 16
     win, oth, lst, nxt = T.wa, T.wb, T.la, T.lb
-    c1, c2 = conv([ra, f], T.cva, 0, B), conv([rb], T.cvb, B, P)
-    op("s", ia[:1], lambda: s.activation(T.wb[:, 0:h2], T.wa[:, 0:h2], CP))
-    ka = widen("s", [ra], win, 0, B)
-    ib = op("s", ia[1:], lambda: s.activation(T.wb[:, h2:H], T.wa[:, h2:H], CP))
-    ready = [ka, widen("v", [rb], win, B, kb), widen("s", [rb], win, kb, P)] + ia
+    c1, c2 = conv([r[0], f], T.cva, win, 0, B), conv(r[-1:], T.cvb, win, B, P)
+    ready = r[-1:] + ia
     cols = ((0, BC), (BC, full))
-    first = (cols, (("g", 0, 0, B), ("v", 1, B, kb), ("s", 1, kb, P)), 1)
-    later = (((LW, full), (0, LW)), (("g", 0, W, W + 512), ("v", 1, 0, w2), ("s", 1, w2, W), ("s", 0, W + 512, W + 640), ("v", 0, W + 640, P)), 0)
-    for (a, b), spec, extra in (first, later, later, later):
+    later = ((LW, full), (0, LW))
+    for i, (a, b) in enumerate((cols, later, later, later)):
         e1 = emit(c1, lst, cols[0][0], cols[0][1], T.cva)
-        t1 = jump(ready + [e1], T.r, 16 * a[0], win, lst, a[0], a[1]) if a == cols[0] else None
+        t1 = jump(ready + [e1], oth, H + 16 * a[0], win, lst, a[0], a[1]) if i != 1 else None
         e2 = emit(c2, lst, cols[1][0], cols[1][1], T.cvb)
         if t1 is None:
-            t1 = jump(ready + [e1, e2], T.r, 16 * a[0], win, lst, a[0], a[1])
-        c1 = conv(t1, T.cva, 16 * a[0], 16 * a[1])
-        t2 = jump([e2], T.r, 16 * b[0], win, lst, b[0], b[1])
-        c2 = conv(t2, T.cvb, 16 * b[0], 16 * b[1])
-        ready = [widen(q, (t1, t2)[w], oth, x, z) for q, w, x, z in spec] + [ib]
+            t1 = jump(ready + [e1, e2], oth, H + 16 * a[0], win, lst, a[0], a[1])
+        c1 = conv(t1, T.cva, oth, 16 * a[0], 16 * a[1])
+        t2 = jump([e2], oth, H + 16 * b[0], win, lst, b[0], b[1])
+        c2 = conv(t2, T.cvb, oth, 16 * b[0], 16 * b[1])
+        ready = t1 + t2
         win, oth = oth, win
-        for _ in range(extra):
-            ready = jump(ready, oth, H, win, lst, 0, full)
+        if i == 0:
+            ready = jump(ready + [ib], oth, H, win, lst, 0, full)
             win, oth = oth, win
         lst, nxt = nxt, lst
         cols = (a, b)
     e1 = emit(c1, lst, cols[0][0], cols[0][1], T.cva)
-    t = jump(ready + [e1], T.r, W, win, lst, LW, full)
-    cp = conv(t, T.cva, W, P)
+    t = jump(ready + [e1], oth, H + W, win, lst, LW, full)
+    cp = conv(t, T.cva, oth, W, P)
     e2 = emit(c2, lst, cols[1][0], cols[1][1], T.cvb)
-    t = jump([e2], T.r, 0, win, lst, 0, LW)
-    cq = conv(t, T.cvb, 0, W)
+    t = jump([e2], oth, H, win, lst, 0, LW)
+    cq = conv(t, T.cvb, oth, 0, W)
     tail = emit(cp, T.ol, LW, full, T.cva)
     te = []
     if not mixed:

from concourse.bass import DstId, RemoteDMATransfer
from concourse.mybir import AluOpType, ActivationFunctionType

N, P, NT, W = 6, 1536, 192, 768
H = NT + W
C = NT // 16
LW = W // 16
B = P // 3
K = 256
CT, LT, TT, IA, IB = 0, 4, 7, 8, 9
SCRATCH = {
    "lnb": ("sbuf", [128, C], "int32"), "dsr": ("sbuf", [128, NT], "int32"),
    "sc": ("sbuf", [128, C], "float32"), "sch": ("sbuf", [128, 1], "float16"),
    "lasts": ("sbuf", [128, C], "uint16"), "ci": ("sbuf", [128, C + 1], "int32"), "cl": ("sbuf", [128, C + 2], "uint16"),
    "pi": ("sbuf", [128, 1], "int32"), "pj": ("sbuf", [128, 1], "int32"), "pf": ("sbuf", [128, 1], "float32"),
    "cut": ("sbuf", [128, 1], "float32"), "p12": ("sbuf", [128, 1], "float32"), "pm": ("sbuf", [128, 1], "float32"),
    "mc": ("sbuf", [128, 1], "float32"), "mt": ("sbuf", [128, 1], "float32"),
    "ma": ("sbuf", [128, 1], "float32"), "mb": ("sbuf", [128, 1], "float32"),
    "ck": ("sbuf", [128, 10], "float32"), "cb": ("sbuf", [128, 10], "float32"),
    "ones": ("sbuf", [128, K], "bfloat16"), "cnt": ("sbuf", [128, K], "bfloat16"),
    "e0": ("sbuf", [128, 132], "float16"), "e1": ("sbuf", [128, 132], "float16"),
    "qp": ("sbuf", [128, 132], "float16"), "qn": ("sbuf", [128, 132], "float16"),
    "gt": ("sbuf", [128, 128], "float16"), "tri": ("sbuf", [128, 128], "float16"),
    "f0": ("sbuf", [128, 144], "bfloat16"), "f1": ("sbuf", [128, 144], "bfloat16"), "f": ("sbuf", [128, 144], "bfloat16"),
    "lt": ("sbuf", [128, NT], "bfloat16"), "ct": ("sbuf", [128, NT], "bfloat16"),
    "rd": ("sbuf", [128, NT + 16], "float16"), "z": ("sbuf", [128, NT], "bfloat16"),
    "d0": ("sbuf", [128, B], "bfloat16"), "d1": ("sbuf", [128, P], "bfloat16"),
    "wa": ("sbuf", [128, H + P], "bfloat16"), "wb": ("sbuf", [128, H + P], "bfloat16"),
    "la": ("sbuf", [128, P // 16], "uint16"), "lb": ("sbuf", [128, P // 16], "uint16"), "ol": ("sbuf", [128, P // 16], "uint16"),
    "idi": ("sbuf", [128, LW], "int32"), "idl": ("sbuf", [128, LW], "uint16"),
    "ll": ("sbuf", [128, N * LW], "uint16"), "cl5": ("sbuf", [128, N * LW], "uint16"),
    "yo": ("sbuf", [128, P], "bfloat16"), "ye": ("sbuf", [128, P], "bfloat16"),
    "dle": ("dram", [2, 128, NT // 2], "bfloat16"), "lel": ("dram", [N, 128, NT // 2], "bfloat16"),
    "car": ("psum", [128, 512], "float32"), "zp": ("psum", [128, 512], "float32"), "ini": ("psum", [128, 512], "float32"),
    "cva": ("psum", [128, 512], "float32"), "cvb": ("psum", [128, 512], "float32"),
}
for _k in range(N):
    SCRATCH["sw%d" % _k] = ("sbuf", [128, H], "bfloat16")
SEMAPHORES = ["cg", "cv", "cs", "cp", "dl", "dd", "dle", "lo", "lw", "lz", "st", "ls"]
SEMAPHORES += ["ar%d" % k for k in range(N)] + ["la%d" % k for k in range(N)]


def rank_program(g, core, T, topo):
    rank = T.rank_of(core)
    if rank is None:
        return
    A, CP, ID = AluOpType, ActivationFunctionType.Copy, ActivationFunctionType.Identity
    v, s, pe, sync, S = g.vector, g.scalar, g.tensor, g.sync, T.sem
    queue = {"g": g, "v": v, "s": s, "p": pe, "y": sync}
    cnt = {"g": 0, "v": 0, "s": 0, "p": 0}
    seen = {}

    def need(q, *deps):
        for sem, val in deps:
            if seen.get((q, sem), 0) < val:
                queue[q].wait_ge(S[sem], val)
                seen[(q, sem)] = val

    def op(q, deps, ins):
        need(q, *deps)
        cnt[q] += 1
        ins().then_inc(S["c" + q], 1)
        return ("c" + q, cnt[q])

    def ts(out, in0, s1, s2, *ops):
        return lambda: v.tensor_scalar(out, in0, s1, s2, *ops)

    up, down = rank, N - 1 - rank
    n = max(up, down)
    mixed = up > 0 and down > 0
    others = [r for r in range(N) if r != rank]
    others.sort(key=lambda r: -abs(r - rank))
    stage = [(k - (n - up), k - (n - down)) for k in range(n)]
    stage = [(a if a >= 0 else None, N - 1 - b if b >= 0 else None) for a, b in stage]
    own = None if mixed else stage[0].index(None)
    sw = [T["sw%d" % k] for k in range(n + 1)]

    def half(side):
        return slice(64 * side, 64 * side + 64)

    sync.dma_start(T.lnb[:], T.ln[:]).then_inc(S.dl, 16)
    dz = op("v", [], lambda: v.memset(T.dsr[:], 0))
    need("y", dz)
    need("s", dz)
    sync.dma_start(T.dsr[CT:128:16, :], T.ds[:]).then_inc(S.dd, 16)
    s.dma_start(T.dsr[CT + 1:128:16, :], T.ds[:]).then_inc(S.dd, 16)
    sync.dma_start(T.dsr[CT + 2:128:16, :], T.ds[:]).then_inc(S.dd, 16)
    sync.dma_start(T.dle[:], T.le[:]).then_inc(S.dle, 16)
    sync.dma_start(sw[n][:, 0:NT], T.le[:]).then_inc(S.lo, 16)
    if not mixed:
        sync.dma_start(sw[0][half(own), 0:NT], T.le[half(own), :]).then_inc(S.lo, 16)

    flag = {"allow_small_or_imprecise_dtypes": True}
    pi = op("g", [], lambda: g.iota(T.pi[:], [[1, 1]], 0, 1))
    ci = op("g", [], lambda: g.iota(T.ci[:], [[1, C + 1]], 0, 0))
    pf = op("g", [], lambda: g.iota(T.pf[:], [[1, 1]], 0, 1, **flag))
    ck = op("g", [], lambda: g.iota(T.ck[:], [[K, 10]], 0, 0, **flag))
    lt = op("g", [], lambda: g.iota(T.lt[:], [[1, C], [C, 16]], 0, 0, **flag))
    ones = op("v", [], lambda: v.memset(T.ones[:], 1.0))
    pj = op("v", [pi], ts(T.pj[:], T.pi[:], 15, None, A.bitwise_and))
    co = op("v", [ones], lambda: v.tensor_tensor_scan(T.cnt[:], T.ones[:], T.ones[:], -1.0, A.add, A.mult))
    mc = op("v", [pj], ts(T.mc[:], T.pj[:], float(CT + 3), None, A.is_lt))
    p12 = op("v", [], ts(T.p12[:], T.pj[:], float(C), None, A.mult))
    cut = op("v", [], ts(T.cut[:], T.pj[:], -float(K), None, A.mult))
    gt = op("v", [co, pf], ts(T.gt[:], T.cnt[:, 0:128], T.pf[:], None, A.is_gt))
    cl = op("v", [p12, ci], ts(T.cl[:, 0:C + 1], T.ci[:], T.p12[:], float(NT - 1), A.add, A.min))
    op("v", [], ts(T.e0[:], T.cnt[:, 0:132], T.pf[:], float(LT), A.subtract, A.is_equal))
    e1 = op("v", [], ts(T.e1[:], T.cnt[:, 0:132], T.pf[:], float(LT - 1), A.subtract, A.is_equal))
    ma = op("v", [], ts(T.ma[:], T.pj[:], float(IA), None, A.is_equal))
    mb = op("v", [], ts(T.mb[:], T.pj[:], float(IB), None, A.is_equal))
    qp = op("v", [e1], lambda: v.tensor_tensor(T.qp[:], T.e0[:], T.e1[:], A.subtract))
    cb = op("v", [mb, ck], ts(T.cb[:], T.ck[:], T.mb[:], None, A.mult))
    qn = op("v", [qp], ts(T.qn[:], T.qp[:], -1.0, None, A.mult))
    mt = op("v", [], ts(T.mt[:], T.pj[:], float(TT), None, A.is_equal))
    tri = op("g", [gt], lambda: g.affine_select(T.tri[:], T.gt[:], [[-16, 8], [0, 16]], A.is_ge, 0.0, 0, 1))
    f0 = op("g", [ones], lambda: g.affine_select(T.f0[:], T.ones[:, 0:144], [[-16, 9], [-4096, 16]], A.is_ge, 0.0, 16, 1))
    f1 = op("g", [f0], lambda: g.affine_select(T.f1[:], T.f0[:], [[16, 9], [-4096, 16]], A.is_ge, 0.0, 14 - 16, -1))
    f = op("g", [f1], lambda: g.affine_select(T.f[:], T.f1[:], [[-16, 9], [0, 16]], A.not_equal, 0.0, 16 - (CT + 3), 1))
    idi = op("g", [], lambda: g.iota(T.idi[:], [[16, LW]], NT, 0)) if mixed else None

    def columns(q, deps, out, o, a, b):
        while a < b:
            k, e = a // K, min(b, (a // K + 1) * K)
            src = T.cnt[:, a - K * k:e - K * k]
            if q == "v":
                t = op(q, deps, ts(out[:, o:o + e - a], src, T.ma[:], T.cb[:, k:k + 1], A.mult, A.add))
            else:
                t = op(q, deps, lambda: s.activation(out[:, o:o + e - a], src, ID, T.cb[:, k:k + 1], T.ma[:]))
            o, a = o + e - a, e
        return t

    dc = [op("s", [mc, ones], lambda: s.activation(T.d0[:, x:x + K], T.ones[:], CP, scale=T.mc[:])) for x in (0, K)][-1]
    x1 = columns("s", [co, ma, cb], T.d1, 1280 - H, 1280, 2048)
    sc = op("v", [("dl", 16), ones], lambda: v.tensor_tensor_scan(T.sc[:], T.lnb[:], T.ones[:, 0:C], 0.0, A.add, A.add))
    rd = op("v", [cl, cut, ("dd", 48)], ts(T.rd[:], T.dsr[:, 0:NT].indirect(T.cl[:, 0:C + 1]), T.cut[:], 0.0, A.add, A.max))
    sch = op("v", [sc], lambda: v.tensor_copy(T.sch[:], T.sc[:, C - 1:C]))
    car = op("p", [tri, sch], lambda: pe.matmul(T.car[:, 0:1], T.tri[:], T.sch[:], True, True))
    ct = op("v", [lt, mt], ts(T.ct[:], T.lt[:], T.mt[:], None, A.mult))
    columns("v", [cb], T.d1, 0, H, 1280)
    lasts = op("v", [car, sc], ts(T.lasts[:], T.sc[:], T.car[:, 0:1], -1.0, A.add, A.add))
    x0 = columns("v", [], T.d1, 2048 - H, 2048, H + P)
    op("p", [qn, rd], lambda: pe.matmul(T.zp[:, 0:NT], T.qn[:, LT:LT + 128], T.rd[:, 16:NT + 16], True, False))
    op("p", [], lambda: pe.matmul(T.zp[:, 0:NT], T.qp[:, LT:LT + 128], T.rd[:, 0:NT], False, False))
    zp = op("p", [], lambda: pe.matmul(T.zp[:, 0:NT], T.qp[:, 0:128], T.rd[:, 16:NT + 16], False, True))
    ini = op("p", [], lambda: pe.matmul(T.ini[:, 0:1], T.qn[:, LT:LT + 128], T.rd[:, 0:1], True, True))
    z = op("v", [zp, ct], lambda: v.tensor_tensor(T.z[:], T.zp[:, 0:NT], T.ct[:], A.add))
    zs = op("v", [z, lasts, x0, x1], lambda: v.tensor_copy(T.d1[:, 0:P].indirect(T.lasts[:, 0:C]), T.z[:]))
    r = []
    for a in range(0, P, B):
        r.append(op("v", r[-1:] if r else [zs, dc, ini], lambda: v.tensor_tensor_scan(
            T.wa[:, H + a:H + a + B], T.d0[:], T.d1[:, a:a + B], T.wa[:, H + a - 1:H + a] if a else T.ini[:, 0:1], A.mult, A.add)))
    ia = [columns("v", [], T.wa, 0, 0, 2 * K), columns("s", [], T.wa, 2 * K, 2 * K, H)]
    ib = columns("s", [], T.wb, 0, 0, H)

    def ids(rs):
        out = []
        for r in rs:
            a = topo.addr(T.cores[r])
            out.append(DstId(rid=a[0], pnc=a[1]))
        return out

    def bits(engines):
        return sum(1 << e for e in engines)

    def shared(src):
        es = [topo.engines(T.cores[src], T.cores[r]) for r in range(N) if r != src]
        return [e for e in es[0] if all(e in x for x in es)]

    def letter_engines(src):
        e = shared(src)
        if src == 0:
            return e, []
        if src == N - 1:
            return [], e
        return e[:len(e) // 2], e[len(e) // 2:]

    trs = []
    for side, rs in ((0, [r for r in others if r > rank]), (1, [r for r in others if r < rank])):
        if rs:
            trs.append(RemoteDMATransfer(dst_ids=ids(rs), dma_engine_mask=bits(letter_engines(rank)[side]), remote_sem=S["la%d" % rank],
                                         srcs=[T.dle[side]], dsts=[T.lel[rank] for _ in rs]))
    g.wait_ge(S.dle, 16)
    g.remote_dma_fused(trs, local_sem=S.ls)
    sent = sum(len(e) for e in letter_engines(rank))

    blank = [(k, side) for k in range(n) for side in range(2) if stage[k][side] is None]
    zero = blank if mixed else blank[1:]
    need("y", op("v", [], lambda: v.memset(T.yo[:, 0:W], 0.0)))
    sync.dma_start(sw[0][:, NT:H], T.yo[:, 0:W]).then_inc(S.lz, 16)
    for k, side in zero:
        sync.dma_start(sw[k][half(side), 0:NT], T.yo[half(side), 0:NT]).then_inc(S.lz, 16)
    z0 = ("lz", 16 + 16 * len(zero) + (16 * len(blank) if mixed else 0))
    if mixed:
        pm = op("v", [], lambda: v.tensor_copy(T.pm[:], T.pj[:]))
        need("y", op("v", [idi, pm], ts(T.idl[:], T.idi[:], T.pm[:], None, A.add)))
        for k, side in blank:
            sync.dma_start(T.cl5[half(side), LW * k:LW * k + LW], T.idl[half(side), :]).then_inc(S.lz, 16)

    def conv(deps, out, win, a, b):
        need("p", *deps)
        for q in range(16):
            t = op("p", [], lambda: pe.matmul(out[:, a // 16:b // 16], T.f[:, 16 - q:144 - q], win[:, H + a + q:H + b:16], q == 0, q == 15))
        return t

    def emit(dep, out, a, b, src):
        return op("v", [dep], lambda: v.tensor_copy(out[:, a:b], src[:, a:b]))

    def jump(deps, out, o, win, lst, a, b):
        h = (a + b) // 2
        e = o + 16 * (h - a)
        z = win.shape[1]
        t1 = op("v", deps, lambda: v.tensor_copy(out[:, o:e], win[:, 0:z].indirect(lst[:, a:h])))
        t2 = op("s", deps, lambda: s.activation(out[:, e:o + 16 * (b - a)], win[:, 0:z].indirect(lst[:, h:b]), CP))
        return [t1, t2]

    full, BC = P // 16, B // 16
    win, oth, lst, nxt = T.wa, T.wb, T.la, T.lb
    c1, c2 = conv([r[0], f], T.cva, win, 0, B), conv(r[-1:], T.cvb, win, B, P)
    ready = r[-1:] + ia
    cols = ((0, BC), (BC, full))
    later = ((LW, full), (0, LW))
    for i, (a, b) in enumerate((cols, later, later, later)):
        e1 = emit(c1, lst, cols[0][0], cols[0][1], T.cva)
        t1 = jump(ready + [e1], oth, H + 16 * a[0], win, lst, a[0], a[1]) if i != 1 else None
        e2 = emit(c2, lst, cols[1][0], cols[1][1], T.cvb)
        if t1 is None:
            t1 = jump(ready + [e1, e2], oth, H + 16 * a[0], win, lst, a[0], a[1])
        c1 = conv(t1, T.cva, oth, 16 * a[0], 16 * a[1])
        t2 = jump([e2], oth, H + 16 * b[0], win, lst, b[0], b[1])
        c2 = conv(t2, T.cvb, oth, 16 * b[0], 16 * b[1])
        ready = t1 + t2
        win, oth = oth, win
        if i == 0:
            ready = jump(ready + [ib], oth, H, win, lst, 0, full)
            win, oth = oth, win
        lst, nxt = nxt, lst
        cols = (a, b)
    e1 = emit(c1, lst, cols[0][0], cols[0][1], T.cva)
    t = jump(ready + [e1], oth, H + W, win, lst, LW, full)
    cp = conv(t, T.cva, oth, W, P)
    e2 = emit(c2, lst, cols[1][0], cols[1][1], T.cvb)
    t = jump([e2], oth, H, win, lst, 0, LW)
    cq = conv(t, T.cvb, oth, 0, W)
    tail = emit(cp, T.ol, LW, full, T.cva)
    te = []
    if not mixed:
        te += jump([tail, z0, ("lo", 32), ("lw", 16 * (up + down))], T.ye, W, sw[0], T.ol, LW, full)
    head = emit(cq, T.ol, 0, LW, T.cvb)
    if not mixed:
        te += jump([head], T.ye, 0, sw[0], T.ol, 0, LW)

    need("g", tail)
    g.remote_dma_fused([RemoteDMATransfer(dst_ids=ids(others), dma_engine_mask=bits(shared(rank)), remote_sem=S["ar%d" % rank],
                                          srcs=[T.ol[:, LW:full]], dsts=[T.ll[:, LW * rank:LW * rank + LW] for _ in others])], local_sem=S.ls)
    sent += len(shared(rank))

    for k in range(n):
        for side in range(2):
            src = stage[k][side]
            if src is not None:
                need("y", ("la%d" % src, len(letter_engines(src)[side])))
                sync.dma_start(sw[k][half(side), 0:NT], T.lel[src]).then_inc(S.lw, 16)
    stored = 0
    if not mixed:
        need("y", *te)
        sync.dma_start(T.y[half(own), :], T.ye[half(own), :]).then_inc(S.st, 16)
        stored += 16

    ready = [z0, ("lw", 16 * (up + down))]
    for k in range(n):
        if mixed:
            for side in range(2):
                src = stage[k][side]
                if src is not None:
                    ready.append(op("v", [("ar%d" % src, len(shared(src)))], lambda: v.tensor_copy(
                        T.cl5[half(side), LW * k:LW * k + LW], T.ll[half(side), LW * src:LW * src + LW])))
            lst, a = T.cl5, LW * k
        else:
            src = stage[k][1 - own]
            ready.append(("ar%d" % src, len(shared(src))))
            lst, a = T.ll, LW * src
        ready = jump(ready, sw[k + 1], NT, sw[k], lst, a, a + LW)
    ready += [head, ("lo", 16 if mixed else 32)]
    rows = slice(0, 128) if mixed else half(1 - own)
    for a, b in ((0, 32), (32, 64), (64, 96)):
        t = jump(ready, T.yo, 16 * a, sw[n], T.ol, a, b)
        need("y", *t)
        sync.dma_start(T.y[rows, 16 * a:16 * b], T.yo[rows, 16 * a:16 * b]).then_inc(S.st, 16)
        stored += 16
    g.wait_ge(S.ls, sent)
    need("y", ("st", stored), *[("c" + q, cnt[q]) for q in cnt])
